import numpy as np, ml_dtypes
CORES = [3,5,19,21,35,37,51,53,67,69]
N = 10
import mx_ref
NC, G, MB = 256, 4, 2
C = np.float32(0.043)
BF = ml_dtypes.bfloat16
def cut(t, i, w=512):
    return t[:, w * i:w * i + w]
def tile(rs):
    return np.stack(rs, axis=2).reshape(128, -1).astype(BF)
def layer(w, X):
    out = []
    for i in range(G):
        for t in range(len(X)):
            p = mx_ref.matmul(mx_ref.quantize(cut(w, len(X) * i + t)), X[t])
            z = p if t == 0 else z + p
        out.append(z)
    return out
def act(Z):
    return [np.maximum(z, 0) * C for z in Z]
def setup_inputs(rng):
    def f(*shape):
        return mx_ref.flush((rng.standard_normal(shape, dtype=np.float32) * np.exp2(rng.integers(-2, 3, shape[:-1] + (1,)))).astype(BF))
    return {"x": f(N, 128, 4 * NC), "w1": f(N, 128, G * 512), "w2": f(N, 128, 512), "px": f(N, 128, MB * 4 * NC), "pw": f(N, 128, G * 512)}
def setup_inputs_blocks(rng):
    d = setup_inputs(rng)
    for k in ("x", "w1", "w2", "px"): d[k] = mx_ref.spread(d[k], rng, 4)
    for k in ("pw",): d[k] = mx_ref.spread(d[k], rng, 1)
    return d
def setup_inputs_wide(rng):
    d = setup_inputs(rng)
    for k in ("x", "w1", "w2", "px"): d[k] = mx_ref.flush((d[k].astype(np.float32) * np.exp2(rng.integers(-6, 7, (N, 1, 1))).astype(np.float32)).astype(BF))
    return d
def setup_inputs_zeros(rng):
    d = setup_inputs(rng); v = d["x"].reshape(N, 128, -1, 4).copy()
    v[np.broadcast_to((rng.random((N, 1, v.shape[2], 1)) < 0.33), v.shape)] = 0
    d["x"] = v.reshape(d["x"].shape)
    return d
def reference(x, w1, w2, px, pw):
    H = [mx_ref.quantize(tile(act(layer(w1[j], [mx_ref.quantize(x[j])])))) for j in range(N)]
    y = np.zeros((N, 128, N * NC), np.float32)
    for r in range(N):
        qw = mx_ref.quantize(w2[r])
        for j in range(N):
            y[r][:, NC * j:NC * j + NC] = mx_ref.matmul(qw, H[j])
    z = np.full((N, 128, MB * G * NC), np.nan, np.float32)
    for m in range(MB):
        a = mx_ref.quantize(cut(px[N - 1], m, 4 * NC))
        for s in range(N - 1):
            a = mx_ref.quantize(tile(act(layer(pw[s], [a]))))
        Z = layer(pw[N - 1], [a])
        for i in range(G):
            z[N - 1][:, NC * (G * m + i):NC * (G * m + i) + NC] = Z[i]
    return {"y": y, "z": z}

@@ -1,0 +1,264 @@
+from concourse.bass import DstId, RemoteDMATransfer
+from concourse.mybir import dt, AluOpType, ActivationFunctionType
+
+N, NC, B, SIM_CORES = 10, 256, 128, 80
+CF = 0.043
+
+
+def mode(to, m):
+    return 2
+
+
+SCRATCH = {
+    "xin": ("sbuf", [128, 1024], "bfloat16"), "w1in": ("sbuf", [128, 2048], "bfloat16"),
+    "w2in": ("sbuf", [128, 512], "bfloat16"), "pwin": ("sbuf", [128, 2048], "bfloat16"),
+    "pxin": ("sbuf", [128, 2048], "bfloat16"),
+    "ht": ("sbuf", [128, 1024], "bfloat16"), "t1": ("sbuf", [128, 1024], "bfloat16"), "t2": ("sbuf", [128, 1024], "bfloat16"),
+    "ybuf": ("sbuf", [128, N * NC], "float32"), "zbuf": ("sbuf", [128, 8 * NC], "float32"),
+    "ps": ("psum", [128, 4096], "float32"),
+}
+for _n, _w in (("x", 256), ("w1", 512), ("w2", 128), ("pw", 512), ("pf", 512), ("px", 512), ("h", N * NC),
+               ("c0", 512), ("c1", 256), ("c2", 512)):
+    SCRATCH[_n + "q"] = ("sbuf", [128, _w], "float8_e4m3fn_x4")
+    SCRATCH[_n + "s"] = ("sbuf", [128, _w], "uint8")
+
+SEMAPHORES = (["l_px0", "l_px1", "l_pwa", "l_pwb", "l_x", "l_w1", "l_w2", "td", "vd", "sd", "st", "sent", "pf"]
+              + ["c%d%d" % (m, b) for m in range(2) for b in range(2)]
+              + ["ga%d" % k for k in range(N // 2)] + ["hi%d" % j for j in range(N)])
+
+
+def hop_plan(how):
+    if how == 2: return [("q", 0, 256, 0), ("s", 0, 256, 0)]
+    if how == 3: return [("q", 0, 128, 0), ("q", 128, 256, 0), ("s", 0, 256, 0)]
+    return [("q", 0, 128, 0), ("s", 0, 128, 0), ("q", 128, 256, 1), ("s", 128, 256, 1)]
+
+
+def bits(mask):
+    return bin(mask).count("1")
+
+
+def rank_program(g, core, T, topo):
+    ranks = list(T.cores)
+    rank = T.rank_of(core)
+    chips = []
+    for c in ranks:
+        if topo.chip(c) not in chips: chips.append(topo.chip(c))
+    groups = [[j for j in range(N) if topo.chip(ranks[j]) == ch] for ch in chips]
+    last = len(groups) - 1
+    sent = [0]
+
+    def in_helper(j, ch):
+        d = topo.die(ranks[j])
+        others = [i for i in range(N) if topo.die(ranks[i]) == d and topo.chip(ranks[i]) != ch]
+        pool = [c for c in range(SIM_CORES) if topo.chip(c) == ch and topo.die(c) == d and c not in ranks]
+        return pool[others.index(j) % len(pool)]
+
+    def far(j):
+        return ranks[[i for i in range(N) if topo.chip(ranks[i]) != topo.chip(ranks[j])][0]]
+
+    def sib(j):
+        return [i for i in range(N) if i != j and topo.chip(ranks[i]) == topo.chip(ranks[j])][0]
+
+    def swap_mask(j):
+        full = topo.mask(ranks[j], ranks[sib(j)])
+        return full if j in groups[0] else full & ~topo.mask(ranks[j], far(j))
+
+    def view(name, kind, a, b):
+        return T[name + "q"][:, a:b].bitcast(dt.uint8) if kind == "q" else T[name + "s"][:, a:b]
+
+    def send(dname, d0, sname, s0, width, kind, dsts, mask, rsem):
+        dst, src = view(dname, kind, d0, d0 + width), view(sname, kind, s0, s0 + width)
+        if len(dsts) == 1:
+            rid, pid, _ = topo.addr(dsts[0])
+            g.remote_dma(dst, src, T.sem[rsem], T.sem["sent"], pid, rid, mask)
+        else:
+            ids = [DstId(rid=topo.addr(d)[0], pnc=topo.addr(d)[1]) for d in dsts]
+            g.remote_dma_fused([RemoteDMATransfer(dst_ids=ids, dma_engine_mask=mask, remote_sem=T.sem[rsem],
+                                                  srcs=[src], dsts=[dst] * len(dsts))], local_sem=T.sem["sent"])
+        sent[0] += bits(mask)
+
+    if rank is None:
+        ch = topo.chip(core)
+        ins = [j for j in reversed(range(N)) if ch in chips and topo.chip(ranks[j]) != ch and in_helper(j, ch) == core]
+        for j in ins:
+            dsts = [c for c in ranks if topo.chip(c) == ch]
+            g.wait_ge(T.sem["hi%d" % j], 2 * bits(topo.mask(ranks[j], core)))
+            for kind in "qs":
+                send("h", NC * j, "h", NC * j, NC, kind, dsts, topo.mask(core, dsts[0]), "ga%d" % (j // 2))
+        if sent[0]: g.wait_ge(T.sem["sent"], sent[0])
+        return
+
+    k = [i for i in range(len(groups)) if rank in groups[i]][0]
+    lane = groups[k].index(rank)
+    final = rank == N - 1
+    sibling = ranks[sib(rank)]
+    queue = {"t": g.tensor, "v": g.vector, "s": g.scalar, "y": g.sync, "g": g}
+    cnt = {"td": 0, "vd": 0, "sd": 0}
+    seen = {}
+    busy = {}
+    stores = [0]
+
+    def need(q, deps):
+        for sem, val in deps:
+            if seen.get((q, sem), 0) < val:
+                queue[q].wait_ge(T.sem[sem], val)
+                seen[(q, sem)] = val
+
+    def done(ins, sem):
+        cnt[sem] += 1
+        ins.then_inc(T.sem[sem], 1)
+        return (sem, cnt[sem])
+
+    def load(sem, dst, src):
+        g.sync.dma_start(dst, src).then_inc(T.sem[sem], 16)
+        return [(sem, 16)]
+
+    def store(dst, src, deps):
+        need("y", deps)
+        g.sync.dma_start(dst, src).then_inc(T.sem["st"], 16)
+        stores[0] += 16
+
+    def quant(name, a, b, src, s0, deps):
+        need("v", deps)
+        return done(g.vector.quantize_mx(T[name + "q"][:, a:b], T[name + "s"][:, a:b], T[src][:, s0:s0 + 4 * (b - a)]), "vd")
+
+    def mm(bank, w, i, src, s0, n, deps):
+        need("t", deps + busy.get(bank, []))
+        return done(g.tensor.matmul_mx(T.ps[:, 512 * bank:512 * bank + n],
+                                       T[w + "q"][:, B * i:B * i + B], T[w + "s"][:, B * i:B * i + B],
+                                       T[src + "q"][:, s0:s0 + n], T[src + "s"][:, s0:s0 + n], True, True), "td")
+
+    def copy(bank, n, dst, d, q):
+        need(q, [d])
+        z = T.ps[:, 512 * bank:512 * bank + n]
+        if q == "s": a = done(g.scalar.activation(dst, z, ActivationFunctionType.Copy), "sd")
+        else: a = done(g.vector.tensor_copy(dst, z), "vd")
+        busy[bank] = [a]
+        return a
+
+    def layer(w, src, s0, deps, n, tile, t0, out, o0, bank):
+        acts = []
+        for i in range(4):
+            d = mm(bank + i, w, i, src, s0, n, deps)
+            dst, z = T[tile][:, t0 + i:t0 + 4 * n:4], T.ps[:, 512 * (bank + i):512 * (bank + i) + n]
+            if i % 2 == 0:
+                need("s", [d])
+                a = done(g.scalar.activation(dst, z, ActivationFunctionType.Relu, scale=CF), "sd")
+            else:
+                need("v", [d])
+                a = done(g.vector.tensor_scalar(dst, z, 0.0, CF, AluOpType.max, AluOpType.mult), "vd")
+            busy[bank + i] = [a]
+            acts.append(a)
+        return quant(out, o0, o0 + n, tile, t0, acts)
+
+    def hop_deps(m, blk):
+        if final: src, to = ranks[groups[last][0]], last + 1
+        elif k == 0: src, to = ranks[N - 1], 0
+        else: src, to = ranks[groups[k - 1][m]], k
+        plan = hop_plan(mode(to, m))
+        if all(p[3] != blk for p in plan): blk = 0
+        return [("c%d%d" % (m, blk), bits(topo.mask(src, core)) * len([p for p in plan if p[3] == blk]))]
+
+    def hop_send(m, name, to, dst, ready):
+        for kind, a, b, blk in hop_plan(mode(to, m)):
+            need("g", [ready[0] if b <= B else ready[1]])
+            send("c0", NC * m + a, name, NC * m + a, b - a, kind, [dst], topo.mask(core, dst), "c%d%d" % (m, blk))
+
+    if final:
+        lpx = [load("l_px%d" % m, T.pxin[:, 1024 * m:1024 * m + 1024], T.px[:, 1024 * m:1024 * m + 1024]) for m in range(2)]
+    if k == 0:
+        lpw = [load("l_pwa", T.pwin[:, 0:1024], T.pw[:, 0:1024]), load("l_pwb", T.pwin[:, 1024:2048], T.pw[:, 1024:2048])]
+    lx = load("l_x", T.xin[:], T.x[:])
+    lw1 = load("l_w1", T.w1in[:], T.w1[:])
+    if k == last: lw2 = load("l_w2", T.w2in[:], T.w2[:])
+    if k != 0: lpw = [load("l_pwa", T.pwin[:], T.pw[:])]
+    if k != last: lw2 = load("l_w2", T.w2in[:], T.w2[:])
+
+    def make_h():
+        quant("x", 0, NC, "xin", 0, lx)
+        dw = quant("w1", 0, 512, "w1in", 0, lw1)
+        d = layer("w1", "x", 0, [dw], NC, "ht", 0, "h", NC * rank, 0)
+        need("g", [d])
+        dsts = [in_helper(rank, ch) for ch in chips[k + 1:] + chips[:k]] + [sibling]
+        for kind in "qs":
+            send("h", NC * rank, "h", NC * rank, NC, kind, dsts, topo.mask(core, dsts[0]), "hi%d" % rank)
+        return d
+
+    def make_pw():
+        if k == 0:
+            for a in (0, NC):
+                d = quant("pw", a, a + NC, "pwin", 4 * a, lpw[a // NC])
+                need("g", [d])
+                send("pf", a, "pw", a, NC, "q", [sibling], swap_mask(rank), "pf")
+            send("pf", 0, "pw", 0, 2 * NC, "s", [sibling], swap_mask(rank), "pf")
+        else:
+            d = quant("pw", 0, 2 * NC, "pwin", 0, lpw[0])
+            if k != last:
+                need("g", [d])
+                for kind in "qs":
+                    send("pf", 0, "pw", 0, 2 * NC, kind, [sibling], swap_mask(rank), "pf")
+        return [d]
+
+    def make_y(dh):
+        dw = quant("w2", 0, B, "w2in", 0, lw2)
+        for n, i in enumerate([k] + [i for i in reversed(range(last + 1)) if i != k]):
+            if i == k: deps = [dw, dh, ("hi%d" % sib(rank), 2 * bits(topo.mask(sibling, far(rank))))]
+            else: deps = [dw, ("ga%d" % i, sum(2 * bits(topo.mask(in_helper(j, topo.chip(core)), core)) for j in groups[i]))]
+            bank = n % 8
+            d = mm(bank, "w2", 0, "h", 2 * NC * i, 2 * NC, deps)
+            a = copy(bank, 2 * NC, T.ybuf[:, 512 * i:512 * i + 512], d, "sv"[n % 2])
+            store(T.y[:, 512 * i:512 * i + 512], T.ybuf[:, 512 * i:512 * i + 512], [a])
+
+    def chain_two(dpw):
+        m = lane
+        own, foreign = ("pw", dpw), ("pf", [("pf", (3 if k == 0 else 2) * bits(swap_mask(sib(rank))))])
+        first, second = (own, foreign) if lane == 0 else (foreign, own)
+        mid = [layer(first[0], "c0", NC * m + B * b, first[1] + hop_deps(m, b), B, "t1", 512 * b, "c1", B * b, 4 * b)
+               for b in range(2)]
+        end = [layer(second[0], "c1", B * b, second[1] + [mid[b]], B, "t2", 512 * b, "c2", NC * m + B * b, 4 * b)
+               for b in range(2)]
+        hop_send(m, "c2", k + 1, ranks[groups[k + 1][lane if k + 1 < last else 0]], end)
+
+    def chain_one(dpw):
+        for m in range(2):
+            end = [layer("pw", "c0", NC * m + B * b, dpw + hop_deps(m, b), B, "t%d" % (m + 1), 512 * b, "c2", NC * m + B * b, 4 * b)
+                   for b in range(2)]
+            hop_send(m, "c2", last + 1, ranks[N - 1], end)
+
+    def chain_z(dpw):
+        for m in range(2):
+            w = B if mode(last + 1, m) == 4 else NC
+            a = {}
+            for b in range(NC // w):
+                for i in range(4):
+                    bank = 4 * ((m if w == NC else b) % 2) + i
+                    d = mm(bank, "pw", i, "c0", NC * m + w * b, w, dpw + hop_deps(m, b))
+                    o = NC * (4 * m + i) + w * b
+                    a[i, b] = copy(bank, w, T.zbuf[:, o:o + w], d, "sv"[i % 2])
+            for half in range(2):
+                o = 1024 * m + 512 * half
+                store(T.z[:, o:o + 512], T.zbuf[:, o:o + 512], [a[i, b] for i in (2 * half, 2 * half + 1) for b in range(NC // w)])
+
+    if final:
+        for m in range(2):
+            d = quant("px", NC * m, NC * m + NC, "pxin", 1024 * m, lpx[m])
+            hop_send(m, "px", 0, ranks[groups[0][m]], [d, d])
+        dh = make_h()
+        dpw = make_pw()
+        make_y(dh)
+        chain_z(dpw)
+    elif k == last:
+        dh = make_h()
+        dpw = make_pw()
+        make_y(dh)
+        chain_one(dpw)
+    elif k == 0:
+        chain_two(make_pw())
+        make_y(make_h())
+    else:
+        dh = make_h()
+        chain_two(make_pw())
+        make_y(dh)
+    g.wait_ge(T.sem["sent"], sent[0])
+    need("g", [(s, cnt[s]) for s in ("td", "vd", "sd")])
+    g.sync.wait_ge(T.sem["st"], stores[0])

@@ -6,7 +6,7 @@ CF = 0.043
 
 
 def mode(to, m):
-    return 2
+    return 4 if to > 0 else 3 - m
 
 
 SCRATCH = {
@@ -22,7 +22,8 @@ for _n, _w in (("x", 256), ("w1", 512), ("w2", 128), ("pw", 512), ("pf", 512), (
     SCRATCH[_n + "q"] = ("sbuf", [128, _w], "float8_e4m3fn_x4")
     SCRATCH[_n + "s"] = ("sbuf", [128, _w], "uint8")
 
-SEMAPHORES = (["l_px0", "l_px1", "l_pwa", "l_pwb", "l_x", "l_w1", "l_w2", "td", "vd", "sd", "st", "sent", "pf"]
+SEMAPHORES = (["l_px0", "l_px1", "l_px2", "l_pwa", "l_pwb", "l_x", "l_w1", "l_w2", "td", "vd", "sd", "st",
+               "sent", "early", "hop", "pf"]
               + ["c%d%d" % (m, b) for m in range(2) for b in range(2)]
               + ["ga%d" % k for k in range(N // 2)] + ["hi%d" % j for j in range(N)])
 
@@ -45,13 +46,17 @@ def rank_program(g, core, T, topo):
         if topo.chip(c) not in chips: chips.append(topo.chip(c))
     groups = [[j for j in range(N) if topo.chip(ranks[j]) == ch] for ch in chips]
     last = len(groups) - 1
-    sent = [0]
+    sent = {"early": 0, "hop": 0, "sent": 0}
 
     def in_helper(j, ch):
         d = topo.die(ranks[j])
         others = [i for i in range(N) if topo.die(ranks[i]) == d and topo.chip(ranks[i]) != ch]
         pool = [c for c in range(SIM_CORES) if topo.chip(c) == ch and topo.die(c) == d and c not in ranks]
         return pool[others.index(j) % len(pool)]
+
+    def via(j):
+        i = chips.index(topo.chip(ranks[j]))
+        return None if i < 2 else chips[last] if i != last else chips[last - 1]
 
     def far(j):
         return ranks[[i for i in range(N) if topo.chip(ranks[i]) != topo.chip(ranks[j])][0]]
@@ -66,26 +71,31 @@ def rank_program(g, core, T, topo):
     def view(name, kind, a, b):
         return T[name + "q"][:, a:b].bitcast(dt.uint8) if kind == "q" else T[name + "s"][:, a:b]
 
-    def send(dname, d0, sname, s0, width, kind, dsts, mask, rsem):
+    def send(dname, d0, sname, s0, width, kind, dsts, mask, rsem, lsem="sent"):
         dst, src = view(dname, kind, d0, d0 + width), view(sname, kind, s0, s0 + width)
         if len(dsts) == 1:
             rid, pid, _ = topo.addr(dsts[0])
-            g.remote_dma(dst, src, T.sem[rsem], T.sem["sent"], pid, rid, mask)
+            g.remote_dma(dst, src, T.sem[rsem], T.sem[lsem], pid, rid, mask)
         else:
             ids = [DstId(rid=topo.addr(d)[0], pnc=topo.addr(d)[1]) for d in dsts]
             g.remote_dma_fused([RemoteDMATransfer(dst_ids=ids, dma_engine_mask=mask, remote_sem=T.sem[rsem],
-                                                  srcs=[src], dsts=[dst] * len(dsts))], local_sem=T.sem["sent"])
-        sent[0] += bits(mask)
+                                                  srcs=[src], dsts=[dst] * len(dsts))], local_sem=T.sem[lsem])
+        sent[lsem] += bits(mask)
 
     if rank is None:
         ch = topo.chip(core)
         ins = [j for j in reversed(range(N)) if ch in chips and topo.chip(ranks[j]) != ch and in_helper(j, ch) == core]
         for j in ins:
             dsts = [c for c in ranks if topo.chip(c) == ch]
-            g.wait_ge(T.sem["hi%d" % j], 2 * bits(topo.mask(ranks[j], core)))
+            src = in_helper(j, via(j)) if ch == chips[1] and via(j) is not None else ranks[j]
+            g.wait_ge(T.sem["hi%d" % j], 2 * bits(topo.mask(src, core)))
             for kind in "qs":
                 send("h", NC * j, "h", NC * j, NC, kind, dsts, topo.mask(core, dsts[0]), "ga%d" % (j // 2))
-        if sent[0]: g.wait_ge(T.sem["sent"], sent[0])
+            if via(j) == ch:
+                dst = in_helper(j, chips[1])
+                for kind in "qs":
+                    send("h", NC * j, "h", NC * j, NC, kind, [dst], topo.mask(core, dst), "hi%d" % j)
+        if sent["sent"]: g.wait_ge(T.sem["sent"], sent["sent"])
         return
 
     k = [i for i in range(len(groups)) if rank in groups[i]][0]
@@ -162,29 +172,46 @@ def rank_program(g, core, T, topo):
     def hop_send(m, name, to, dst, ready):
         for kind, a, b, blk in hop_plan(mode(to, m)):
             need("g", [ready[0] if b <= B else ready[1]])
-            send("c0", NC * m + a, name, NC * m + a, b - a, kind, [dst], topo.mask(core, dst), "c%d%d" % (m, blk))
+            send("c0", NC * m + a, name, NC * m + a, b - a, kind, [dst], topo.mask(core, dst), "c%d%d" % (m, blk),
+                 "hop" if to else "early" if m == 0 else "sent")
 
     if final:
-        lpx = [load("l_px%d" % m, T.pxin[:, 1024 * m:1024 * m + 1024], T.px[:, 1024 * m:1024 * m + 1024]) for m in range(2)]
-    if k == 0:
+        lpx = [load("l_px0", T.pxin[:, 0:512], T.px[:, 0:512]), load("l_px1", T.pxin[:, 512:1024], T.px[:, 512:1024]),
+               load("l_px2", T.pxin[:, 1024:2048], T.px[:, 1024:2048])]
+    elif k == 0:
         lpw = [load("l_pwa", T.pwin[:, 0:1024], T.pw[:, 0:1024]), load("l_pwb", T.pwin[:, 1024:2048], T.pw[:, 1024:2048])]
-    lx = load("l_x", T.xin[:], T.x[:])
-    lw1 = load("l_w1", T.w1in[:], T.w1[:])
-    if k == last: lw2 = load("l_w2", T.w2in[:], T.w2[:])
-    if k != 0: lpw = [load("l_pwa", T.pwin[:], T.pw[:])]
-    if k != last: lw2 = load("l_w2", T.w2in[:], T.w2[:])
+        lx = load("l_x", T.xin[:], T.x[:])
+    else:
+        lx = load("l_x", T.xin[:], T.x[:])
+        lw1 = load("l_w1", T.w1in[:], T.w1[:])
+        if k == last: lw2 = load("l_w2", T.w2in[:], T.w2[:])
+        lpw = [load("l_pwa", T.pwin[:], T.pw[:])]
+        if k != last: lw2 = load("l_w2", T.w2in[:], T.w2[:])
 
-    def make_h():
+    def more_loads(gate):
+        need("y", [(gate, sent[gate])])
+        d = {}
+        if final: d["x"] = load("l_x", T.xin[:], T.x[:])
+        d["w1"] = load("l_w1", T.w1in[:], T.w1[:])
+        d["w2"] = load("l_w2", T.w2in[:], T.w2[:])
+        if final: d["pw"] = [load("l_pwa", T.pwin[:], T.pw[:])]
+        return d
+
+    def make_h(lx, lw1):
         quant("x", 0, NC, "xin", 0, lx)
         dw = quant("w1", 0, 512, "w1in", 0, lw1)
         d = layer("w1", "x", 0, [dw], NC, "ht", 0, "h", NC * rank, 0)
         need("g", [d])
-        dsts = [in_helper(rank, ch) for ch in chips[k + 1:] + chips[:k]] + [sibling]
-        for kind in "qs":
-            send("h", NC * rank, "h", NC * rank, NC, kind, dsts, topo.mask(core, dsts[0]), "hi%d" % rank)
+        if k == 0: to = chips[:0:-1]
+        elif k == last: to = chips[:1] + chips[last - 1:1:-1]
+        else: to = chips[k + 1:] + chips[2:k] + chips[:1]
+        dsts = [in_helper(rank, ch) for ch in to] + [sibling]
+        for part in (dsts[:1], dsts[1:]) if k == 0 else (dsts,):
+            for kind in "qs":
+                send("h", NC * rank, "h", NC * rank, NC, kind, part, topo.mask(core, dsts[0]), "hi%d" % rank)
         return d
 
-    def make_pw():
+    def make_pw(lpw):
         if k == 0:
             for a in (0, NC):
                 d = quant("pw", a, a + NC, "pwin", 4 * a, lpw[a // NC])
@@ -199,9 +226,11 @@ def rank_program(g, core, T, topo):
                     send("pf", 0, "pw", 0, 2 * NC, kind, [sibling], swap_mask(rank), "pf")
         return [d]
 
-    def make_y(dh):
-        dw = quant("w2", 0, B, "w2in", 0, lw2)
-        for n, i in enumerate([k] + [i for i in reversed(range(last + 1)) if i != k]):
+    def make_w2(lw2):
+        return quant("w2", 0, B, "w2in", 0, lw2)
+
+    def make_y(dh, dw, which):
+        for n, i in which:
             if i == k: deps = [dw, dh, ("hi%d" % sib(rank), 2 * bits(topo.mask(sibling, far(rank))))]
             else: deps = [dw, ("ga%d" % i, sum(2 * bits(topo.mask(in_helper(j, topo.chip(core)), core)) for j in groups[i]))]
             bank = n % 8
@@ -239,26 +268,34 @@ def rank_program(g, core, T, topo):
                 o = 1024 * m + 512 * half
                 store(T.z[:, o:o + 512], T.zbuf[:, o:o + 512], [a[i, b] for i in (2 * half, 2 * half + 1) for b in range(NC // w)])
 
+    order = list(enumerate([k] + [i for i in reversed(range(last + 1)) if i != k]))
     if final:
         for m in range(2):
-            d = quant("px", NC * m, NC * m + NC, "pxin", 1024 * m, lpx[m])
-            hop_send(m, "px", 0, ranks[groups[0][m]], [d, d])
-        dh = make_h()
-        dpw = make_pw()
-        make_y(dh)
+            if m == 0: d = [quant("px", 0, B, "pxin", 0, lpx[0]), quant("px", B, NC, "pxin", 512, lpx[1])]
+            else: d = [quant("px", NC, 2 * NC, "pxin", 1024, lpx[2])] * 2
+            hop_send(m, "px", 0, ranks[groups[0][m]], d)
+        rest = more_loads("early")
+        dh = make_h(rest["x"], rest["w1"])
+        dw, dpw = make_w2(rest["w2"]), make_pw(rest["pw"])
+        make_y(dh, dw, order)
         chain_z(dpw)
     elif k == last:
-        dh = make_h()
-        dpw = make_pw()
-        make_y(dh)
+        dh = make_h(lx, lw1)
+        dw, dpw = make_w2(lw2), make_pw(lpw)
+        make_y(dh, dw, order[:3])
         chain_one(dpw)
+        need("y", [("hop", sent["hop"])])
+        make_y(dh, dw, order[3:])
     elif k == 0:
-        chain_two(make_pw())
-        make_y(make_h())
+        chain_two(make_pw(lpw))
+        rest = more_loads("hop")
+        dh = make_h(lx, rest["w1"])
+        make_y(dh, make_w2(rest["w2"]), order)
     else:
-        dh = make_h()
-        chain_two(make_pw())
-        make_y(dh)
-    g.wait_ge(T.sem["sent"], sent[0])
+        dh = make_h(lx, lw1)
+        chain_two(make_pw(lpw))
+        need("y", [("hop", sent["hop"])])
+        make_y(dh, make_w2(lw2), order)
+    need("g", [(s, v) for s, v in sent.items() if v])
     need("g", [(s, cnt[s]) for s in ("td", "vd", "sd")])
     g.sync.wait_ge(T.sem["st"], stores[0])

from concourse.bass import DstId, RemoteDMATransfer
from concourse.mybir import dt, AluOpType, ActivationFunctionType

N, NC, B, SIM_CORES = 10, 256, 128, 80
CF = 0.043


def mode(to, m):
    return 4 if to > 0 else 3 - m


SCRATCH = {
    "xin": ("sbuf", [128, 1024], "bfloat16"), "w1in": ("sbuf", [128, 2048], "bfloat16"),
    "w2in": ("sbuf", [128, 512], "bfloat16"), "pwin": ("sbuf", [128, 2048], "bfloat16"),
    "pxin": ("sbuf", [128, 2048], "bfloat16"),
    "ht": ("sbuf", [128, 1024], "bfloat16"), "t1": ("sbuf", [128, 1024], "bfloat16"), "t2": ("sbuf", [128, 1024], "bfloat16"),
    "ybuf": ("sbuf", [128, N * NC], "float32"), "zbuf": ("sbuf", [128, 8 * NC], "float32"),
    "ps": ("psum", [128, 4096], "float32"),
}
for _n, _w in (("x", 256), ("w1", 512), ("w2", 128), ("pw", 512), ("pf", 512), ("px", 512), ("h", N * NC),
               ("c0", 512), ("c1", 256), ("c2", 512)):
    SCRATCH[_n + "q"] = ("sbuf", [128, _w], "float8_e4m3fn_x4")
    SCRATCH[_n + "s"] = ("sbuf", [128, _w], "uint8")

SEMAPHORES = (["l_px0", "l_px1", "l_px2", "l_pwa", "l_pwb", "l_x", "l_w1", "l_w2", "td", "vd", "sd", "st",
               "sent", "early", "hop", "pf"]
              + ["c%d%d" % (m, b) for m in range(2) for b in range(2)]
              + ["ga%d" % k for k in range(N // 2)] + ["hi%d" % j for j in range(N)])


def hop_plan(how):
    if how == 2: return [("q", 0, 256, 0), ("s", 0, 256, 0)]
    if how == 3: return [("q", 0, 128, 0), ("q", 128, 256, 0), ("s", 0, 256, 0)]
    return [("q", 0, 128, 0), ("s", 0, 128, 0), ("q", 128, 256, 1), ("s", 128, 256, 1)]


def bits(mask):
    return bin(mask).count("1")


def rank_program(g, core, T, topo):
    ranks = list(T.cores)
    rank = T.rank_of(core)
    chips = []
    for c in ranks:
        if topo.chip(c) not in chips: chips.append(topo.chip(c))
    groups = [[j for j in range(N) if topo.chip(ranks[j]) == ch] for ch in chips]
    last = len(groups) - 1
    sent = {"early": 0, "hop": 0, "sent": 0}

    def in_helper(j, ch):
        d = topo.die(ranks[j])
        others = [i for i in range(N) if topo.die(ranks[i]) == d and topo.chip(ranks[i]) != ch]
        pool = [c for c in range(SIM_CORES) if topo.chip(c) == ch and topo.die(c) == d and c not in ranks]
        return pool[others.index(j) % len(pool)]

    def via(j):
        i = chips.index(topo.chip(ranks[j]))
        return None if i < 2 else chips[last] if i != last else chips[last - 1]

    def far(j):
        return ranks[[i for i in range(N) if topo.chip(ranks[i]) != topo.chip(ranks[j])][0]]

    def sib(j):
        return [i for i in range(N) if i != j and topo.chip(ranks[i]) == topo.chip(ranks[j])][0]

    def swap_mask(j):
        full = topo.mask(ranks[j], ranks[sib(j)])
        return full if j in groups[0] else full & ~topo.mask(ranks[j], far(j))

    def view(name, kind, a, b):
        return T[name + "q"][:, a:b].bitcast(dt.uint8) if kind == "q" else T[name + "s"][:, a:b]

    def send(dname, d0, sname, s0, width, kind, dsts, mask, rsem, lsem="sent"):
        dst, src = view(dname, kind, d0, d0 + width), view(sname, kind, s0, s0 + width)
        if len(dsts) == 1:
            rid, pid, _ = topo.addr(dsts[0])
            g.remote_dma(dst, src, T.sem[rsem], T.sem[lsem], pid, rid, mask)
        else:
            ids = [DstId(rid=topo.addr(d)[0], pnc=topo.addr(d)[1]) for d in dsts]
            g.remote_dma_fused([RemoteDMATransfer(dst_ids=ids, dma_engine_mask=mask, remote_sem=T.sem[rsem],
                                                  srcs=[src], dsts=[dst] * len(dsts))], local_sem=T.sem[lsem])
        sent[lsem] += bits(mask)

    if rank is None:
        ch = topo.chip(core)
        ins = [j for j in reversed(range(N)) if ch in chips and topo.chip(ranks[j]) != ch and in_helper(j, ch) == core]
        for j in ins:
            dsts = [c for c in ranks if topo.chip(c) == ch]
            src = in_helper(j, via(j)) if ch == chips[1] and via(j) is not None else ranks[j]
            g.wait_ge(T.sem["hi%d" % j], 2 * bits(topo.mask(src, core)))
            for kind in "qs":
                send("h", NC * j, "h", NC * j, NC, kind, dsts, topo.mask(core, dsts[0]), "ga%d" % (j // 2))
            if via(j) == ch:
                dst = in_helper(j, chips[1])
                for kind in "qs":
                    send("h", NC * j, "h", NC * j, NC, kind, [dst], topo.mask(core, dst), "hi%d" % j)
        if sent["sent"]: g.wait_ge(T.sem["sent"], sent["sent"])
        return

    k = [i for i in range(len(groups)) if rank in groups[i]][0]
    lane = groups[k].index(rank)
    final = rank == N - 1
    sibling = ranks[sib(rank)]
    queue = {"t": g.tensor, "v": g.vector, "s": g.scalar, "y": g.sync, "g": g}
    cnt = {"td": 0, "vd": 0, "sd": 0}
    seen = {}
    busy = {}
    stores = [0]

    def need(q, deps):
        for sem, val in deps:
            if seen.get((q, sem), 0) < val:
                queue[q].wait_ge(T.sem[sem], val)
                seen[(q, sem)] = val

    def done(ins, sem):
        cnt[sem] += 1
        ins.then_inc(T.sem[sem], 1)
        return (sem, cnt[sem])

    def load(sem, dst, src):
        g.sync.dma_start(dst, src).then_inc(T.sem[sem], 16)
        return [(sem, 16)]

    def store(dst, src, deps):
        need("y", deps)
        g.sync.dma_start(dst, src).then_inc(T.sem["st"], 16)
        stores[0] += 16

    def quant(name, a, b, src, s0, deps):
        need("v", deps)
        return done(g.vector.quantize_mx(T[name + "q"][:, a:b], T[name + "s"][:, a:b], T[src][:, s0:s0 + 4 * (b - a)]), "vd")

    def mm(bank, w, i, src, s0, n, deps):
        need("t", deps + busy.get(bank, []))
        return done(g.tensor.matmul_mx(T.ps[:, 512 * bank:512 * bank + n],
                                       T[w + "q"][:, B * i:B * i + B], T[w + "s"][:, B * i:B * i + B],
                                       T[src + "q"][:, s0:s0 + n], T[src + "s"][:, s0:s0 + n], True, True), "td")

    def copy(bank, n, dst, d, q):
        need(q, [d])
        z = T.ps[:, 512 * bank:512 * bank + n]
        if q == "s": a = done(g.scalar.activation(dst, z, ActivationFunctionType.Copy), "sd")
        else: a = done(g.vector.tensor_copy(dst, z), "vd")
        busy[bank] = [a]
        return a

    def layer(w, src, s0, deps, n, tile, t0, out, o0, bank):
        acts = []
        for i in range(4):
            d = mm(bank + i, w, i, src, s0, n, deps)
            dst, z = T[tile][:, t0 + i:t0 + 4 * n:4], T.ps[:, 512 * (bank + i):512 * (bank + i) + n]
            if i % 2 == 0:
                need("s", [d])
                a = done(g.scalar.activation(dst, z, ActivationFunctionType.Relu, scale=CF), "sd")
            else:
                need("v", [d])
                a = done(g.vector.tensor_scalar(dst, z, 0.0, CF, AluOpType.max, AluOpType.mult), "vd")
            busy[bank + i] = [a]
            acts.append(a)
        return quant(out, o0, o0 + n, tile, t0, acts)

    def hop_deps(m, blk):
        if final: src, to = ranks[groups[last][0]], last + 1
        elif k == 0: src, to = ranks[N - 1], 0
        else: src, to = ranks[groups[k - 1][m]], k
        plan = hop_plan(mode(to, m))
        if all(p[3] != blk for p in plan): blk = 0
        return [("c%d%d" % (m, blk), bits(topo.mask(src, core)) * len([p for p in plan if p[3] == blk]))]

    def hop_send(m, name, to, dst, ready):
        for kind, a, b, blk in hop_plan(mode(to, m)):
            need("g", [ready[0] if b <= B else ready[1]])
            send("c0", NC * m + a, name, NC * m + a, b - a, kind, [dst], topo.mask(core, dst), "c%d%d" % (m, blk),
                 "hop" if to else "early" if m == 0 else "sent")

    if final:
        lpx = [load("l_px0", T.pxin[:, 0:512], T.px[:, 0:512]), load("l_px1", T.pxin[:, 512:1024], T.px[:, 512:1024]),
               load("l_px2", T.pxin[:, 1024:2048], T.px[:, 1024:2048])]
    elif k == 0:
        lpw = [load("l_pwa", T.pwin[:, 0:1024], T.pw[:, 0:1024]), load("l_pwb", T.pwin[:, 1024:2048], T.pw[:, 1024:2048])]
        lx = load("l_x", T.xin[:], T.x[:])
    else:
        lx = load("l_x", T.xin[:], T.x[:])
        lw1 = load("l_w1", T.w1in[:], T.w1[:])
        if k == last: lw2 = load("l_w2", T.w2in[:], T.w2[:])
        lpw = [load("l_pwa", T.pwin[:], T.pw[:])]
        if k != last: lw2 = load("l_w2", T.w2in[:], T.w2[:])

    def more_loads(gate):
        need("y", [(gate, sent[gate])])
        d = {}
        if final: d["x"] = load("l_x", T.xin[:], T.x[:])
        d["w1"] = load("l_w1", T.w1in[:], T.w1[:])
        d["w2"] = load("l_w2", T.w2in[:], T.w2[:])
        if final: d["pw"] = [load("l_pwa", T.pwin[:], T.pw[:])]
        return d

    def make_h(lx, lw1):
        quant("x", 0, NC, "xin", 0, lx)
        dw = quant("w1", 0, 512, "w1in", 0, lw1)
        d = layer("w1", "x", 0, [dw], NC, "ht", 0, "h", NC * rank, 0)
        need("g", [d])
        if k == 0: to = chips[:0:-1]
        elif k == last: to = chips[:1] + chips[last - 1:1:-1]
        else: to = chips[k + 1:] + chips[2:k] + chips[:1]
        dsts = [in_helper(rank, ch) for ch in to] + [sibling]
        for part in (dsts[:1], dsts[1:]) if k == 0 else (dsts,):
            for kind in "qs":
                send("h", NC * rank, "h", NC * rank, NC, kind, part, topo.mask(core, dsts[0]), "hi%d" % rank)
        return d

    def make_pw(lpw):
        if k == 0:
            for a in (0, NC):
                d = quant("pw", a, a + NC, "pwin", 4 * a, lpw[a // NC])
                need("g", [d])
                send("pf", a, "pw", a, NC, "q", [sibling], swap_mask(rank), "pf")
            send("pf", 0, "pw", 0, 2 * NC, "s", [sibling], swap_mask(rank), "pf")
        else:
            d = quant("pw", 0, 2 * NC, "pwin", 0, lpw[0])
            if k != last:
                need("g", [d])
                for kind in "qs":
                    send("pf", 0, "pw", 0, 2 * NC, kind, [sibling], swap_mask(rank), "pf")
        return [d]

    def make_w2(lw2):
        return quant("w2", 0, B, "w2in", 0, lw2)

    def make_y(dh, dw, which):
        for n, i in which:
            if i == k: deps = [dw, dh, ("hi%d" % sib(rank), 2 * bits(topo.mask(sibling, far(rank))))]
            else: deps = [dw, ("ga%d" % i, sum(2 * bits(topo.mask(in_helper(j, topo.chip(core)), core)) for j in groups[i]))]
            bank = n % 8
            d = mm(bank, "w2", 0, "h", 2 * NC * i, 2 * NC, deps)
            a = copy(bank, 2 * NC, T.ybuf[:, 512 * i:512 * i + 512], d, "sv"[n % 2])
            store(T.y[:, 512 * i:512 * i + 512], T.ybuf[:, 512 * i:512 * i + 512], [a])

    def chain_two(dpw):
        m = lane
        own, foreign = ("pw", dpw), ("pf", [("pf", (3 if k == 0 else 2) * bits(swap_mask(sib(rank))))])
        first, second = (own, foreign) if lane == 0 else (foreign, own)
        mid = [layer(first[0], "c0", NC * m + B * b, first[1] + hop_deps(m, b), B, "t1", 512 * b, "c1", B * b, 4 * b)
               for b in range(2)]
        end = [layer(second[0], "c1", B * b, second[1] + [mid[b]], B, "t2", 512 * b, "c2", NC * m + B * b, 4 * b)
               for b in range(2)]
        hop_send(m, "c2", k + 1, ranks[groups[k + 1][lane if k + 1 < last else 0]], end)

    def chain_one(dpw):
        for m in range(2):
            end = [layer("pw", "c0", NC * m + B * b, dpw + hop_deps(m, b), B, "t%d" % (m + 1), 512 * b, "c2", NC * m + B * b, 4 * b)
                   for b in range(2)]
            hop_send(m, "c2", last + 1, ranks[N - 1], end)

    def chain_z(dpw):
        for m in range(2):
            w = B if mode(last + 1, m) == 4 else NC
            a = {}
            for b in range(NC // w):
                for i in range(4):
                    bank = 4 * ((m if w == NC else b) % 2) + i
                    d = mm(bank, "pw", i, "c0", NC * m + w * b, w, dpw + hop_deps(m, b))
                    o = NC * (4 * m + i) + w * b
                    a[i, b] = copy(bank, w, T.zbuf[:, o:o + w], d, "sv"[i % 2])
            for half in range(2):
                o = 1024 * m + 512 * half
                store(T.z[:, o:o + 512], T.zbuf[:, o:o + 512], [a[i, b] for i in (2 * half, 2 * half + 1) for b in range(NC // w)])

    order = list(enumerate([k] + [i for i in reversed(range(last + 1)) if i != k]))
    if final:
        for m in range(2):
            if m == 0: d = [quant("px", 0, B, "pxin", 0, lpx[0]), quant("px", B, NC, "pxin", 512, lpx[1])]
            else: d = [quant("px", NC, 2 * NC, "pxin", 1024, lpx[2])] * 2
            hop_send(m, "px", 0, ranks[groups[0][m]], d)
        rest = more_loads("early")
        dh = make_h(rest["x"], rest["w1"])
        dw, dpw = make_w2(rest["w2"]), make_pw(rest["pw"])
        make_y(dh, dw, order)
        chain_z(dpw)
    elif k == last:
        dh = make_h(lx, lw1)
        dw, dpw = make_w2(lw2), make_pw(lpw)
        make_y(dh, dw, order[:3])
        chain_one(dpw)
        need("y", [("hop", sent["hop"])])
        make_y(dh, dw, order[3:])
    elif k == 0:
        chain_two(make_pw(lpw))
        rest = more_loads("hop")
        dh = make_h(lx, rest["w1"])
        make_y(dh, make_w2(rest["w2"]), order)
    else:
        dh = make_h(lx, lw1)
        chain_two(make_pw(lpw))
        need("y", [("hop", sent["hop"])])
        make_y(dh, make_w2(lw2), order)
    need("g", [(s, v) for s, v in sent.items() if v])
    need("g", [(s, cnt[s]) for s in ("td", "vd", "sd")])
    g.sync.wait_ge(T.sem["st"], stores[0])
